import numpy as np
import ml_dtypes


def mxq(x, axis, fmt="e4m3"):
    dtype, down = {"e4m3": (ml_dtypes.float8_e4m3fn, 7), "e5m2": (ml_dtypes.float8_e5m2, 14)}[fmt]
    v = np.moveaxis(np.asarray(x, np.float32).astype(ml_dtypes.bfloat16).astype(np.float64), axis, -1)
    blocks = v.reshape(v.shape[:-1] + (-1, 32))
    amax = np.abs(blocks).max(-1, keepdims=True)
    byte = np.maximum(np.where(amax > 0, np.frexp(amax)[1] - 1 + 127, 0) - down, 1)
    scale = np.exp2(byte - 127.0)
    codes = (blocks / scale).astype(np.float32).astype(dtype).astype(np.float64)
    return np.moveaxis((codes * scale).reshape(v.shape), -1, axis)


WIDE = False


def mx_kscale(k):
    if not WIDE:
        return np.ones(k)
    levels = np.array([24, -24, 12, -12, 0])
    if k % 512:
        return np.exp2(np.random.permutation(np.resize(levels, k // 32))).repeat(32)
    a = np.empty((k // 512, 16))
    for p in range(k // 512):
        a[p, :8] = np.random.permutation(np.resize(levels, 8))
        for g in range(8):
            far = levels[np.abs(levels - a[p, g]) >= 10]
            a[p, g + 8] = far[np.random.randint(len(far))]
    return np.exp2(a.ravel()).repeat(32)


def f64(x):
    return np.asarray(x).astype(np.float64)


def striped8(idx):
    return np.concatenate([v.reshape(-1, 16).T for v in idx]).astype(np.uint16)


def unstriped8(offs):
    return np.stack([offs[16 * g:16 * g + 16].T.reshape(-1) for g in range(8)]).astype(np.int64)


E2M1 = np.array([0.0, 0.5, 1.0, 1.5, 2.0, 3.0, 4.0, 6.0, -0.0, -0.5, -1.0, -1.5, -2.0, -3.0, -4.0, -6.0])


def pack_weight(w, fmt):
    k, n = w.shape
    w = f64(np.asarray(w, np.float32).astype(ml_dtypes.bfloat16)).reshape(k // 32, 32, n)
    amax = np.abs(w).max(1)
    if fmt == "e4m3":
        byte = np.frexp(amax)[1] - 1 + 127 - 7
    else:
        mant, ex = np.frexp(amax / 6.0)
        byte = np.where(mant > 0.5, ex, ex - 1) + 127
    byte = np.clip(np.where(amax > 0, byte, 1), 1, 254)
    scaled = (w * np.exp2(127.0 - byte)[:, None, :]).reshape(k, n).astype(np.float32)
    by_word = np.ascontiguousarray(scaled.reshape(k // 512, 128, 4, n).transpose(0, 1, 3, 2))
    if fmt == "e4m3":
        words = by_word.astype(ml_dtypes.float8_e4m3fn).view(np.uint8)
    else:
        c = by_word.astype(ml_dtypes.float4_e2m1fn).view(np.uint8) & 0xF
        words = (c[..., 0::2] | (c[..., 1::2] << 4)).reshape(k // 512, 128, 2 * n)
    return np.ascontiguousarray(words), np.ascontiguousarray(byte.astype(np.uint8).reshape(k // 512, 16, n))


def unpack_weight(words, scales, fmt):
    g, _, n = scales.shape
    words = np.ascontiguousarray(words).reshape(g, 128, n, -1)
    if fmt == "e4m3":
        vals = words.view(ml_dtypes.float8_e4m3fn).astype(np.float64)
    else:
        nib = np.empty((g, 128, n, 4), np.uint8)
        nib[..., 0::2] = words & 0xF
        nib[..., 1::2] = words >> 4
        vals = E2M1[nib]
    vals = vals * np.repeat(np.exp2(scales.astype(np.float64) - 127.0), 8, axis=1)[..., None]
    return vals.transpose(0, 1, 3, 2).reshape(g * 512, n)


def planes(y):
    n, m = y.shape
    v = y.astype(np.float32).astype(ml_dtypes.bfloat16).astype(np.float64).reshape(n // 32, 32, m)
    top = np.abs(v).max(1)
    byte = np.clip(np.where(top > 0, np.frexp(top)[1] - 1 + 127 - 7, 1), 1, 254)
    codes = (v * np.exp2(127.0 - byte)[:, None, :]).reshape(n, m).astype(np.float32).astype(ml_dtypes.float8_e4m3fn).view(np.uint8)
    words = codes.reshape(n // 512, 128, 4, m).transpose(0, 1, 3, 2)
    return np.ascontiguousarray(words), np.ascontiguousarray(byte.astype(np.uint8).reshape(n // 512, 16, m))


K, R, N, T, J = 1024, 512, 512, 2048, 1024


def setup_inputs():
    n = np.random.standard_normal
    s = mx_kscale(K)[:, None]
    u = mx_kscale(R)[:, None]
    p_wg = pack_weight(n((K, R)) / np.sqrt(K) / s, "e4m3")
    return {
        "xT": (n((K, T)) * s).astype(np.float32),
        "wgt": np.repeat(np.random.uniform(0.5, 2.0, (8, J)), 16, axis=0).astype(np.float32),
        "wg_words": p_wg[0],
        "wg_scales": p_wg[1],
        "wu": (n((K, R)) / np.sqrt(K) / s * u.T).astype(np.float32),
        "wd": (n((R, N)) / np.sqrt(R) / u).astype(np.float32),
        "b": (0.3 * n(N)).astype(np.float32),
        "offs": striped8(np.stack([np.random.permutation(T)[:J] for _ in range(8)])),
    }


def reference(xT, wgt, wg_words, wg_scales, wu, wd, b, offs):
    idx = unstriped8(offs)
    rows = np.arange(K)
    xg = f64(wgt)[rows // 4 % 128] * f64(xT)[rows[:, None], idx[rows % 512 // 64]]
    xT_ = mxq(xg, 0, "e4m3")
    wg_ = unpack_weight(wg_words, wg_scales, "e4m3")
    wu_ = mxq(f64(wu), 0, "e4m3")
    ga = wg_.T @ xT_
    ub = wu_.T @ xT_
    h = np.tanh(ga) * ub
    h_ = mxq(h, 0, "e4m3")
    wd_ = mxq(f64(wd), 0, "e4m3")
    y = wd_.T @ h_
    out_0 = y + f64(b)[:, None]
    return (out_0,) + planes(out_0)

@@ -1,0 +1,218 @@
+from contextlib import ExitStack
+
+import concourse.mybir as mybir
+
+K, R, N, T, J = 1024, 512, 512, 2048, 1024
+FLOPS = 2 * J * (2 * K * R + R * N)
+
+F32 = mybir.dt.float32
+BF16 = mybir.dt.bfloat16
+I32 = mybir.dt.int32
+U16 = mybir.dt.uint16
+U8 = mybir.dt.uint8
+FP8X4 = mybir.dt.float8_e4m3fn_x4
+MULT = mybir.AluOpType.mult
+TANH = mybir.ActivationFunctionType.Tanh
+IDENTITY = mybir.ActivationFunctionType.Identity
+
+P = 128
+PACK = 4
+PASSES = K // (P * PACK)
+HALF = J // 2
+WIDE = 256
+NARROW = 128
+
+
+def tile_list_tanh_biasP_kernel(
+    tc, xT, wgt, wg_words, wg_scales, wu, wd, b, offs, out_0, out_1, out_2
+):
+    nc = tc.nc
+    with ExitStack() as ctx:
+        keep = ctx.enter_context(tc.tile_pool(name="keep", bufs=1))
+        ring = ctx.enter_context(tc.tile_pool(name="ring", bufs=4))
+        psum = ctx.enter_context(tc.psum_pool(name="psum", bufs=2))
+
+        def held(shape, dtype, name):
+            return keep.tile(shape, dtype, name=name, align_bytes=64)
+
+        wg_s_raw = held([P, R], U8, "wg_s_raw")
+        nc.vector.memset(wg_s_raw[:].bitcast(I32), 0)
+
+        offsets = keep.tile([P, J // 16], U16, name="offsets")
+        nc.sync.dma_start(offsets[:], offs)
+        wgt_sb = held([P, J], F32, "wgt_sb")
+        nc.sync.dma_start(wgt_sb[:], wgt)
+        x_planes = xT.rearrange("(a p i) t -> a i p t", p=P, i=PACK)
+        x_sb = {}
+        for a in range(PASSES):
+            for i in range(PACK):
+                x_sb[a, i] = held([P, T], F32, "x_%d_%d" % (a, i))
+                nc.sync.dma_start(x_sb[a, i][:], x_planes[a, i])
+        wg_w_raw = held([P, PASSES, R], I32, "wg_w_raw")
+        nc.sync.dma_start(wg_w_raw[:], wg_words.rearrange("a p r i -> p a (r i)").bitcast(I32))
+        for q in range(4):
+            nc.sync.dma_start(
+                wg_s_raw[32 * q : 32 * q + 4 * PASSES, :].bitcast(I32),
+                wg_scales[:, 4 * q : 4 * q + 4, :].bitcast(I32),
+            )
+        wu_rows = wu.rearrange("(a p i) r -> a p i r", p=P, i=PACK)
+        wu_raw = []
+        for a in range(PASSES):
+            wu_raw.append(held([P, PACK, R], F32, "wu_raw_%d" % a))
+            nc.sync.dma_start(wu_raw[a][:], wu_rows[a])
+        wd_raw = held([P, PACK, N], F32, "wd_raw")
+        nc.sync.dma_start(wd_raw[:], wd.rearrange("(p i) n -> p i n", i=PACK))
+        bias = held([P, PACK], F32, "bias")
+        nc.sync.dma_start(bias[:], b.rearrange("(p t) -> p t", t=PACK))
+
+        def quantise(codes, scales, values):
+            nc.vector.quantize_mx(out=codes.bitcast(FP8X4), scales=scales, in_=values)
+
+        def interleave(copy, dst, src):
+            copy(
+                dst.rearrange("p (c s t) -> p c t s", s=4, t=PACK),
+                src.rearrange("p t (c s) -> p c t s", s=4),
+            )
+
+        def deal(copy, dst, raw):
+            copy(
+                dst.rearrange("p (t m i) -> p m i t", t=PACK, i=PACK),
+                raw.rearrange("p i (m t) -> p m i t", t=PACK),
+            )
+
+        x_codes = [held([P, J], I32, "x_codes_%d" % a) for a in range(PASSES)]
+        x_scales = [held([P, J], U8, "x_scales_%d" % a) for a in range(PASSES)]
+
+        def round_x(a, src, j0):
+            xb = ring.tile([P, WIDE * PACK], BF16, name="xb", align_bytes=64)
+            interleave(nc.scalar.copy, xb[:], src)
+            return xb
+
+        def quant_x(a, xb, j0):
+            quantise(x_codes[a][:, j0 : j0 + WIDE], x_scales[a][:, j0 : j0 + WIDE], xb[:])
+
+        g0 = held([P, PACK, J], F32, "g0")
+        for i in range(PACK):
+            nc.vector.tensor_tensor(g0[:, i, :], x_sb[0, i][:].indirect(offsets[:]), wgt_sb[:], MULT)
+        xb0 = [round_x(0, g0[:, :, j0 : j0 + WIDE], j0) for j0 in range(0, J, WIDE)]
+        g1 = [held([P, PACK, HALF], F32, "g1_%d" % h) for h in range(2)]
+        for i in range(PACK):
+            for h in range(2):
+                nc.vector.tensor_tensor(
+                    g1[h][:, i, :],
+                    x_sb[1, i][:].indirect(offsets[:, h * HALF // 16 : (h + 1) * HALF // 16]),
+                    wgt_sb[:, h * HALF : (h + 1) * HALF],
+                    MULT,
+                )
+        for c in range(J // WIDE):
+            quant_x(0, xb0[c], c * WIDE)
+
+        wg_codes = held([P, PASSES, R], I32, "wg_codes")
+        nc.vector.tensor_copy(
+            wg_codes[:].rearrange("p a (t m) -> p a m t", t=PACK),
+            wg_w_raw[:].rearrange("p a (m t) -> p a m t", t=PACK),
+        )
+        wg_s = held([P, R], U8, "wg_s")
+        nc.vector.tensor_copy(
+            wg_s[:].rearrange("p (t m) -> p m t", t=PACK),
+            wg_s_raw[:].rearrange("p (m t) -> p m t", t=PACK),
+        )
+
+        for c in range(J // WIDE):
+            j0 = c * WIDE
+            xb = round_x(1, g1[j0 // HALF][:, :, j0 % HALF : j0 % HALF + WIDE], j0)
+            quant_x(1, xb, j0)
+
+        wu_codes = [held([P, R], I32, "wu_codes_%d" % a) for a in range(PASSES)]
+        wu_scales = [held([P, R], U8, "wu_scales_%d" % a) for a in range(PASSES)]
+        for a in range(PASSES):
+            wu_b = held([P, R * PACK], BF16, "wu_b_%d" % a)
+            deal(nc.vector.tensor_copy, wu_b[:], wu_raw[a][:])
+            quantise(wu_codes[a][:], wu_scales[a][:], wu_b[:])
+
+        def first_product(bank, codes, scales, j0):
+            for t in range(PACK):
+                cols = slice(t * P, (t + 1) * P)
+                for a in range(PASSES):
+                    nc.tensor.matmul_mx(
+                        out=bank[:, t, :],
+                        lhsT=codes(a, cols).bitcast(FP8X4),
+                        lhsT_scale=scales(a, cols),
+                        rhs=x_codes[a][:, j0 : j0 + NARROW].bitcast(FP8X4),
+                        rhs_scale=x_scales[a][:, j0 : j0 + NARROW],
+                        start=(a == 0),
+                        stop=(a == PASSES - 1),
+                    )
+
+        wd_b = held([P, N * PACK], BF16, "wd_b")
+        wd_codes = held([P, N], I32, "wd_codes")
+        wd_scales = held([P, N], U8, "wd_scales")
+        gate = []
+        for c in range(J // NARROW):
+            ga = psum.tile([P, PACK, NARROW], F32, name="ga")
+            first_product(ga, lambda a, cols: wg_codes[:, a, cols], lambda a, cols: wg_s[4 * a :, cols], c * NARROW)
+            gate.append(held([P, NARROW, PACK], F32, "gate_%d" % c))
+            nc.scalar.activation(gate[c][:], ga[:].rearrange("p t j -> p j t"), TANH)
+            if c == 3:
+                deal(nc.scalar.copy, wd_b[:], wd_raw[:])
+                quantise(wd_codes[:], wd_scales[:], wd_b[:])
+
+        h_codes = held([P, J], I32, "h_codes")
+        h_scales = held([P, J], U8, "h_scales")
+        y_codes = held([P, J], I32, "y_codes")
+        y_scales = held([P, J], U8, "y_scales")
+        out_rows = out_0.rearrange("(p t) j -> p t j", t=PACK)
+        out_words = out_1[0].rearrange("p j i -> p (j i)").bitcast(I32)
+
+        def hidden(w):
+            hb = ring.tile([P, WIDE, PACK], BF16, name="hb", align_bytes=64, bufs=2)
+            for s in range(WIDE // NARROW):
+                c = w * (WIDE // NARROW) + s
+                ub = psum.tile([P, PACK, NARROW], F32, name="ub")
+                first_product(ub, lambda a, cols: wu_codes[a][:, cols], lambda a, cols: wu_scales[a][:, cols], c * NARROW)
+                nc.vector.tensor_tensor(
+                    hb[:, s * NARROW : (s + 1) * NARROW, :], ub[:].rearrange("p t j -> p j t"), gate[c][:], MULT
+                )
+            js = slice(w * WIDE, (w + 1) * WIDE)
+            quantise(h_codes[:, js], h_scales[:, js], hb[:].rearrange("p j t -> p (j t)"))
+
+        def down(w):
+            js = slice(w * WIDE, (w + 1) * WIDE)
+            yf = ring.tile([P, PACK, WIDE], F32, name="yf", align_bytes=64)
+            for u in range(2):
+                bank = psum.tile([P, 2, WIDE], F32, name="ybank", bufs=4)
+                for v in range(2):
+                    t = 2 * u + v
+                    cols = slice(t * P, (t + 1) * P)
+                    nc.tensor.matmul_mx(
+                        out=bank[:, v, :],
+                        lhsT=wd_codes[:, cols].bitcast(FP8X4),
+                        lhsT_scale=wd_scales[:, cols],
+                        rhs=h_codes[:, js].bitcast(FP8X4),
+                        rhs_scale=h_scales[:, js],
+                        start=True,
+                        stop=True,
+                    )
+                for v in range(2):
+                    t = 2 * u + v
+                    nc.scalar.activation(yf[:, t, :], bank[:, v, :], IDENTITY, bias=bias[:, t : t + 1])
+            nc.sync.dma_start(out_rows[:, :, js], yf[:])
+            return yf
+
+        def planes(w, yf):
+            js = slice(w * WIDE, (w + 1) * WIDE)
+            yb = ring.tile([P, WIDE * PACK], BF16, name="yb", align_bytes=64, bufs=2)
+            interleave(nc.vector.tensor_copy, yb[:], yf[:])
+            quantise(y_codes[:, js], y_scales[:, js], yb[:])
+            nc.sync.dma_start(out_words[:, js], y_codes[:, js])
+
+        ys = []
+        for w in range(J // WIDE):
+            hidden(w)
+            ys.append(down(w))
+        for w in range(J // WIDE):
+            planes(w, ys[w])
+        for q in range(4):
+            nc.sync.dma_start(
+                out_2[0, 4 * q : 4 * q + 4, :].bitcast(I32), y_scales[32 * q : 32 * q + 4, :].bitcast(I32)
+            )

@@ -29,8 +29,7 @@ def tile_list_tanh_biasP_kernel(
     nc = tc.nc
     with ExitStack() as ctx:
         keep = ctx.enter_context(tc.tile_pool(name="keep", bufs=1))
-        ring = ctx.enter_context(tc.tile_pool(name="ring", bufs=4))
-        psum = ctx.enter_context(tc.psum_pool(name="psum", bufs=2))
+        psum = ctx.enter_context(tc.psum_pool(name="psum", bufs=1))
 
         def held(shape, dtype, name):
             return keep.tile(shape, dtype, name=name, align_bytes=64)
@@ -38,32 +37,60 @@ def tile_list_tanh_biasP_kernel(
         wg_s_raw = held([P, R], U8, "wg_s_raw")
         nc.vector.memset(wg_s_raw[:].bitcast(I32), 0)
 
-        offsets = keep.tile([P, J // 16], U16, name="offsets")
-        nc.sync.dma_start(offsets[:], offs)
-        wgt_sb = held([P, J], F32, "wgt_sb")
-        nc.sync.dma_start(wgt_sb[:], wgt)
         x_planes = xT.rearrange("(a p i) t -> a i p t", p=P, i=PACK)
         x_sb = {}
-        for a in range(PASSES):
-            for i in range(PACK):
-                x_sb[a, i] = held([P, T], F32, "x_%d_%d" % (a, i))
-                nc.sync.dma_start(x_sb[a, i][:], x_planes[a, i])
+
+        def load_x(a, i):
+            x_sb[a, i] = held([P, T], F32, "x_%d_%d" % (a, i))
+            nc.sync.dma_start(x_sb[a, i][:], x_planes[a, i])
+
+        wgt_sb = [held([P, HALF], F32, "wgt_%d" % h) for h in range(2)]
+
+        def load_wgt(h):
+            nc.sync.dma_start(wgt_sb[h][:], wgt[:, h * HALF : (h + 1) * HALF])
+
         wg_w_raw = held([P, PASSES, R], I32, "wg_w_raw")
-        nc.sync.dma_start(wg_w_raw[:], wg_words.rearrange("a p r i -> p a (r i)").bitcast(I32))
-        for q in range(4):
-            nc.sync.dma_start(
-                wg_s_raw[32 * q : 32 * q + 4 * PASSES, :].bitcast(I32),
-                wg_scales[:, 4 * q : 4 * q + 4, :].bitcast(I32),
-            )
+
+        def load_wg():
+            nc.sync.dma_start(wg_w_raw[:], wg_words.rearrange("a p r i -> p a (r i)").bitcast(I32))
+            for q in range(4):
+                nc.sync.dma_start(
+                    wg_s_raw[32 * q : 32 * q + 4 * PASSES, :].bitcast(I32),
+                    wg_scales[:, 4 * q : 4 * q + 4, :].bitcast(I32),
+                )
+
         wu_rows = wu.rearrange("(a p i) r -> a p i r", p=P, i=PACK)
-        wu_raw = []
-        for a in range(PASSES):
-            wu_raw.append(held([P, PACK, R], F32, "wu_raw_%d" % a))
+        wu_raw = [held([P, PACK, R], F32, "wu_raw_%d" % a) for a in range(PASSES)]
+
+        def load_wu(a):
             nc.sync.dma_start(wu_raw[a][:], wu_rows[a])
+
         wd_raw = held([P, PACK, N], F32, "wd_raw")
-        nc.sync.dma_start(wd_raw[:], wd.rearrange("(p i) n -> p i n", i=PACK))
         bias = held([P, PACK], F32, "bias")
-        nc.sync.dma_start(bias[:], b.rearrange("(p t) -> p t", t=PACK))
+
+        def load_wd():
+            nc.sync.dma_start(wd_raw[:], wd.rearrange("(p i) n -> p i n", i=PACK))
+
+        def load_bias():
+            nc.sync.dma_start(bias[:], b.rearrange("(p t) -> p t", t=PACK))
+
+        offsets = keep.tile([P, J // 16], U16, name="offsets")
+        nc.sync.dma_start(offsets[:], offs)
+        load_wgt(0)
+        load_x(0, 0)
+        load_wgt(1)
+        load_x(0, 1)
+        load_x(0, 2)
+        load_x(0, 3)
+        load_x(1, 0)
+        load_wg()
+        load_wu(1)
+        load_x(1, 1)
+        load_x(1, 2)
+        load_wu(0)
+        load_x(1, 3)
+        load_wd()
+        load_bias()
 
         def quantise(codes, scales, values):
             nc.vector.quantize_mx(out=codes.bitcast(FP8X4), scales=scales, in_=values)
@@ -80,82 +107,88 @@ def tile_list_tanh_biasP_kernel(
                 raw.rearrange("p i (m t) -> p m i t", t=PACK),
             )
 
+        V = nc.vector.tensor_copy
+        S = nc.scalar.copy
+
         x_codes = [held([P, J], I32, "x_codes_%d" % a) for a in range(PASSES)]
         x_scales = [held([P, J], U8, "x_scales_%d" % a) for a in range(PASSES)]
+        picked = {(a, h): held([P, PACK, HALF], F32, "picked_%d_%d" % (a, h)) for a in range(PASSES) for h in range(2)}
+        xb = {}
 
-        def round_x(a, src, j0):
-            xb = ring.tile([P, WIDE * PACK], BF16, name="xb", align_bytes=64)
-            interleave(nc.scalar.copy, xb[:], src)
-            return xb
+        def gather(a, i, h):
+            nc.vector.tensor_tensor(
+                picked[a, h][:, i, :],
+                x_sb[a, i][:].indirect(offsets[:, h * HALF // 16 : (h + 1) * HALF // 16]),
+                wgt_sb[h][:],
+                MULT,
+            )
 
-        def quant_x(a, xb, j0):
-            quantise(x_codes[a][:, j0 : j0 + WIDE], x_scales[a][:, j0 : j0 + WIDE], xb[:])
+        def round_x(copy, a, j0, width):
+            xb[a, j0] = keep.tile([P, width * PACK], BF16, name="xb_%d" % width, align_bytes=64, bufs=(2 if width == HALF else 4))
+            interleave(copy, xb[a, j0][:], picked[a, j0 // HALF][:, :, j0 % HALF : j0 % HALF + width])
 
-        g0 = held([P, PACK, J], F32, "g0")
-        for i in range(PACK):
-            nc.vector.tensor_tensor(g0[:, i, :], x_sb[0, i][:].indirect(offsets[:]), wgt_sb[:], MULT)
-        xb0 = [round_x(0, g0[:, :, j0 : j0 + WIDE], j0) for j0 in range(0, J, WIDE)]
-        g1 = [held([P, PACK, HALF], F32, "g1_%d" % h) for h in range(2)]
-        for i in range(PACK):
-            for h in range(2):
-                nc.vector.tensor_tensor(
-                    g1[h][:, i, :],
-                    x_sb[1, i][:].indirect(offsets[:, h * HALF // 16 : (h + 1) * HALF // 16]),
-                    wgt_sb[:, h * HALF : (h + 1) * HALF],
-                    MULT,
-                )
-        for c in range(J // WIDE):
-            quant_x(0, xb0[c], c * WIDE)
+        def quant_x(a, j0, width):
+            quantise(x_codes[a][:, j0 : j0 + width], x_scales[a][:, j0 : j0 + width], xb[a, j0][:])
 
         wg_codes = held([P, PASSES, R], I32, "wg_codes")
-        nc.vector.tensor_copy(
-            wg_codes[:].rearrange("p a (t m) -> p a m t", t=PACK),
-            wg_w_raw[:].rearrange("p a (m t) -> p a m t", t=PACK),
-        )
         wg_s = held([P, R], U8, "wg_s")
-        nc.vector.tensor_copy(
-            wg_s[:].rearrange("p (t m) -> p m t", t=PACK),
-            wg_s_raw[:].rearrange("p (m t) -> p m t", t=PACK),
-        )
 
-        for c in range(J // WIDE):
-            j0 = c * WIDE
-            xb = round_x(1, g1[j0 // HALF][:, :, j0 % HALF : j0 % HALF + WIDE], j0)
-            quant_x(1, xb, j0)
+        def deal_wg():
+            nc.vector.tensor_copy(
+                wg_codes[:].rearrange("p a (t m) -> p a m t", t=PACK),
+                wg_w_raw[:].rearrange("p a (m t) -> p a m t", t=PACK),
+            )
+            nc.vector.tensor_copy(
+                wg_s[:].rearrange("p (t m) -> p m t", t=PACK),
+                wg_s_raw[:].rearrange("p (m t) -> p m t", t=PACK),
+            )
 
         wu_codes = [held([P, R], I32, "wu_codes_%d" % a) for a in range(PASSES)]
         wu_scales = [held([P, R], U8, "wu_scales_%d" % a) for a in range(PASSES)]
-        for a in range(PASSES):
-            wu_b = held([P, R * PACK], BF16, "wu_b_%d" % a)
-            deal(nc.vector.tensor_copy, wu_b[:], wu_raw[a][:])
-            quantise(wu_codes[a][:], wu_scales[a][:], wu_b[:])
+        wu_b = [held([P, R * PACK], BF16, "wu_b_%d" % a) for a in range(PASSES)]
+
+        def deal_wu(copy, a):
+            deal(copy, wu_b[a][:], wu_raw[a][:])
+
+        def quant_wu(a):
+            quantise(wu_codes[a][:], wu_scales[a][:], wu_b[a][:])
+
+        wd_b = held([P, N * PACK], BF16, "wd_b")
+        wd_codes = held([P, N], I32, "wd_codes")
+        wd_scales = held([P, N], U8, "wd_scales")
+
+        def deal_wd(copy):
+            deal(copy, wd_b[:], wd_raw[:])
+
+        def quant_wd():
+            quantise(wd_codes[:], wd_scales[:], wd_b[:])
 
         def first_product(bank, codes, scales, j0):
-            for t in range(PACK):
-                cols = slice(t * P, (t + 1) * P)
-                for a in range(PASSES):
+            for a in range(PASSES):
+                for t in range(PACK):
+                    cols = slice(t * P, (t + 1) * P)
                     nc.tensor.matmul_mx(
                         out=bank[:, t, :],
                         lhsT=codes(a, cols).bitcast(FP8X4),
                         lhsT_scale=scales(a, cols),
                         rhs=x_codes[a][:, j0 : j0 + NARROW].bitcast(FP8X4),
                         rhs_scale=x_scales[a][:, j0 : j0 + NARROW],
-                        start=(a == 0),
-                        stop=(a == PASSES - 1),
+                        start=(a == 0 and t == 0),
+                        stop=(a == PASSES - 1 and t == PACK - 1),
                     )
 
-        wd_b = held([P, N * PACK], BF16, "wd_b")
-        wd_codes = held([P, N], I32, "wd_codes")
-        wd_scales = held([P, N], U8, "wd_scales")
-        gate = []
-        for c in range(J // NARROW):
-            ga = psum.tile([P, PACK, NARROW], F32, name="ga")
+        gate = {}
+        banks_taken = []
+
+        def next_bank(shape):
+            banks_taken.append(shape)
+            return psum.tile(shape, F32, name="bank_%d" % ((len(banks_taken) - 1) % 8))
+
+        def tanh(c):
+            ga = next_bank([P, PACK, NARROW])
             first_product(ga, lambda a, cols: wg_codes[:, a, cols], lambda a, cols: wg_s[4 * a :, cols], c * NARROW)
-            gate.append(held([P, NARROW, PACK], F32, "gate_%d" % c))
+            gate[c] = keep.tile([P, NARROW, PACK], F32, name="gate", align_bytes=64, bufs=8)
             nc.scalar.activation(gate[c][:], ga[:].rearrange("p t j -> p j t"), TANH)
-            if c == 3:
-                deal(nc.scalar.copy, wd_b[:], wd_raw[:])
-                quantise(wd_codes[:], wd_scales[:], wd_b[:])
 
         h_codes = held([P, J], I32, "h_codes")
         h_scales = held([P, J], U8, "h_scales")
@@ -163,26 +196,32 @@ def tile_list_tanh_biasP_kernel(
         y_scales = held([P, J], U8, "y_scales")
         out_rows = out_0.rearrange("(p t) j -> p t j", t=PACK)
         out_words = out_1[0].rearrange("p j i -> p (j i)").bitcast(I32)
+        hb = held([P, J * PACK], BF16, "hb")
+        yb = held([P, J * PACK], BF16, "yb")
+        yf = {}
 
-        def hidden(w):
-            hb = ring.tile([P, WIDE, PACK], BF16, name="hb", align_bytes=64, bufs=2)
-            for s in range(WIDE // NARROW):
-                c = w * (WIDE // NARROW) + s
-                ub = psum.tile([P, PACK, NARROW], F32, name="ub")
-                first_product(ub, lambda a, cols: wu_codes[a][:, cols], lambda a, cols: wu_scales[a][:, cols], c * NARROW)
-                nc.vector.tensor_tensor(
-                    hb[:, s * NARROW : (s + 1) * NARROW, :], ub[:].rearrange("p t j -> p j t"), gate[c][:], MULT
-                )
-            js = slice(w * WIDE, (w + 1) * WIDE)
-            quantise(h_codes[:, js], h_scales[:, js], hb[:].rearrange("p j t -> p (j t)"))
+        def hidden(c):
+            ub = next_bank([P, PACK, NARROW])
+            first_product(ub, lambda a, cols: wu_codes[a][:, cols], lambda a, cols: wu_scales[a][:, cols], c * NARROW)
+            nc.vector.tensor_tensor(
+                hb[:, c * NARROW * PACK : (c + 1) * NARROW * PACK].rearrange("p (j t) -> p j t", t=PACK),
+                ub[:].rearrange("p t j -> p j t"),
+                gate[c][:],
+                MULT,
+            )
 
-        def down(w):
-            js = slice(w * WIDE, (w + 1) * WIDE)
-            yf = ring.tile([P, PACK, WIDE], F32, name="yf", align_bytes=64)
-            for u in range(2):
-                bank = psum.tile([P, 2, WIDE], F32, name="ybank", bufs=4)
-                for v in range(2):
-                    t = 2 * u + v
+        def quant_h(j0, width):
+            js = slice(j0, j0 + width)
+            quantise(h_codes[:, js], h_scales[:, js], hb[:, j0 * PACK : (j0 + width) * PACK])
+
+        def down(j0, width):
+            js = slice(j0, j0 + width)
+            yf[j0] = held([P, PACK, width], F32, "yf_%d" % j0)
+            per_bank = min(PACK, 512 // width)
+            for u in range(PACK // per_bank):
+                bank = next_bank([P, per_bank, width])
+                for v in range(per_bank):
+                    t = per_bank * u + v
                     cols = slice(t * P, (t + 1) * P)
                     nc.tensor.matmul_mx(
                         out=bank[:, v, :],
@@ -193,26 +232,91 @@ def tile_list_tanh_biasP_kernel(
                         start=True,
                         stop=True,
                     )
-                for v in range(2):
-                    t = 2 * u + v
-                    nc.scalar.activation(yf[:, t, :], bank[:, v, :], IDENTITY, bias=bias[:, t : t + 1])
-            nc.sync.dma_start(out_rows[:, :, js], yf[:])
-            return yf
+                for v in range(per_bank):
+                    t = per_bank * u + v
+                    nc.scalar.activation(yf[j0][:, t, :], bank[:, v, :], IDENTITY, bias=bias[:, t : t + 1])
+            nc.sync.dma_start(out_rows[:, :, js], yf[j0][:])
 
-        def planes(w, yf):
-            js = slice(w * WIDE, (w + 1) * WIDE)
-            yb = ring.tile([P, WIDE * PACK], BF16, name="yb", align_bytes=64, bufs=2)
-            interleave(nc.vector.tensor_copy, yb[:], yf[:])
-            quantise(y_codes[:, js], y_scales[:, js], yb[:])
+        def round_y(copy, j0, width):
+            interleave(copy, yb[:, j0 * PACK : (j0 + width) * PACK], yf[j0][:])
+
+        def quant_y(j0, width):
+            js = slice(j0, j0 + width)
+            quantise(y_codes[:, js], y_scales[:, js], yb[:, j0 * PACK : (j0 + width) * PACK])
             nc.sync.dma_start(out_words[:, js], y_codes[:, js])
 
-        ys = []
-        for w in range(J // WIDE):
-            hidden(w)
-            ys.append(down(w))
-        for w in range(J // WIDE):
-            planes(w, ys[w])
-        for q in range(4):
-            nc.sync.dma_start(
-                out_2[0, 4 * q : 4 * q + 4, :].bitcast(I32), y_scales[32 * q : 32 * q + 4, :].bitcast(I32)
-            )
+        def store_scales():
+            for q in range(4):
+                queue = nc.sync if q % 2 else nc.scalar
+                queue.dma_start(
+                    out_2[0, 4 * q : 4 * q + 4, :].bitcast(I32), y_scales[32 * q : 32 * q + 4, :].bitcast(I32)
+                )
+
+        gather(0, 0, 0)
+        gather(0, 0, 1)
+        gather(0, 1, 0)
+        gather(0, 1, 1)
+        gather(0, 2, 0)
+        gather(0, 2, 1)
+        gather(0, 3, 0)
+        gather(0, 3, 1)
+        round_x(S, 0, 0, 512)
+        round_x(S, 0, 512, 512)
+        deal_wu(S, 1)
+        deal_wu(S, 0)
+        gather(1, 0, 0)
+        gather(1, 0, 1)
+        deal_wg()
+        gather(1, 1, 0)
+        gather(1, 1, 1)
+        gather(1, 2, 0)
+        gather(1, 2, 1)
+        quant_x(0, 0, 512)
+        quant_x(0, 512, 512)
+        quant_wu(1)
+        gather(1, 3, 0)
+        quant_wu(0)
+        gather(1, 3, 1)
+        round_x(S, 1, 0, 256)
+        quant_x(1, 0, 256)
+        deal_wd(V)
+        round_x(S, 1, 256, 256)
+        quant_x(1, 256, 256)
+        quant_wd()
+        round_x(S, 1, 512, 256)
+        quant_x(1, 512, 256)
+        tanh(0)
+        tanh(1)
+        tanh(2)
+        tanh(3)
+        round_x(S, 1, 768, 256)
+        quant_x(1, 768, 256)
+        hidden(0)
+        hidden(1)
+        quant_h(0, 256)
+        hidden(2)
+        hidden(3)
+        quant_h(256, 256)
+        tanh(4)
+        tanh(5)
+        down(0, 256)
+        round_y(V, 0, 256)
+        quant_y(0, 256)
+        hidden(4)
+        hidden(5)
+        quant_h(512, 256)
+        tanh(6)
+        tanh(7)
+        down(256, 256)
+        round_y(V, 256, 256)
+        quant_y(256, 256)
+        hidden(6)
+        hidden(7)
+        quant_h(768, 256)
+        down(512, 256)
+        round_y(V, 512, 256)
+        quant_y(512, 256)
+        down(768, 256)
+        round_y(V, 768, 256)
+        quant_y(768, 256)
+        store_scales()

@@ -46,8 +46,24 @@ def tile_list_tanh_biasP_kernel(
 
         wgt_sb = [held([P, HALF], F32, "wgt_%d" % h) for h in range(2)]
 
-        def load_wgt(h):
-            nc.sync.dma_start(wgt_sb[h][:], wgt[:, h * HALF : (h + 1) * HALF])
+        wgt_rows = held([P, 64], F32, "wgt_rows")
+
+        def load_L():
+            nc.sync.dma_start(wgt_rows[:], wgt.rearrange("(g r) (s c) -> r g s c", r=16, c=64)[0])
+
+        def prep_wgt():
+            turned = held([P, 64], F32, "wgt_turned")
+            for e in range(2):
+                nc.vector.transpose(turned[:, 32 * e : 32 * (e + 1)], wgt_rows[:, 32 * e : 32 * (e + 1)])
+            by_piece = turned[:].rearrange("p (e u s) -> p s e u", e=2, u=2)
+            spread = [held([P, HALF], F32, "wgt_spread_%d" % h) for h in range(2)]
+            for h in range(2):
+                nc.vector.tensor_copy(
+                    spread[h][:].rearrange("p (s e u k) -> p s e u k", e=2, u=2, k=16),
+                    by_piece[:, 8 * h : 8 * (h + 1)].unsqueeze(4).broadcast_to([P, 8, 2, 2, 16]),
+                )
+            for h in range(2):
+                nc.vector.transpose(wgt_sb[h][:], spread[h][:])
 
         wg_w_raw = held([P, PASSES, R], I32, "wg_w_raw")
 
@@ -76,9 +92,8 @@ def tile_list_tanh_biasP_kernel(
 
         offsets = keep.tile([P, J // 16], U16, name="offsets")
         nc.sync.dma_start(offsets[:], offs)
-        load_wgt(0)
+        load_L()
         load_x(0, 0)
-        load_wgt(1)
         load_x(0, 1)
         load_x(0, 2)
         load_x(0, 3)
@@ -187,7 +202,7 @@ def tile_list_tanh_biasP_kernel(
         def tanh(c):
             ga = next_bank([P, PACK, NARROW])
             first_product(ga, lambda a, cols: wg_codes[:, a, cols], lambda a, cols: wg_s[4 * a :, cols], c * NARROW)
-            gate[c] = keep.tile([P, NARROW, PACK], F32, name="gate", align_bytes=64, bufs=8)
+            gate[c] = keep.tile([P, NARROW, PACK], F32, name="gate", align_bytes=64, bufs=6)
             nc.scalar.activation(gate[c][:], ga[:].rearrange("p t j -> p j t"), TANH)
 
         h_codes = held([P, J], I32, "h_codes")
@@ -252,6 +267,7 @@ def tile_list_tanh_biasP_kernel(
                     out_2[0, 4 * q : 4 * q + 4, :].bitcast(I32), y_scales[32 * q : 32 * q + 4, :].bitcast(I32)
                 )
 
+        prep_wgt()
         gather(0, 0, 0)
         gather(0, 0, 1)
         gather(0, 1, 0)

@@ -44,7 +44,7 @@ def tile_list_tanh_biasP_kernel(
             x_sb[a, i] = held([P, T], F32, "x_%d_%d" % (a, i))
             nc.sync.dma_start(x_sb[a, i][:], x_planes[a, i])
 
-        wgt_sb = [held([P, HALF], F32, "wgt_%d" % h) for h in range(2)]
+        wgt_sb = held([P, J], F32, "wgt_sb")
 
         wgt_rows = held([P, 64], F32, "wgt_rows")
 
@@ -58,12 +58,12 @@ def tile_list_tanh_biasP_kernel(
             by_piece = turned[:].rearrange("p (e u s) -> p s e u", e=2, u=2)
             spread = [held([P, HALF], F32, "wgt_spread_%d" % h) for h in range(2)]
             for h in range(2):
-                nc.vector.tensor_copy(
+                (nc.vector.tensor_copy, nc.scalar.copy)[h](
                     spread[h][:].rearrange("p (s e u k) -> p s e u k", e=2, u=2, k=16),
                     by_piece[:, 8 * h : 8 * (h + 1)].unsqueeze(4).broadcast_to([P, 8, 2, 2, 16]),
                 )
             for h in range(2):
-                nc.vector.transpose(wgt_sb[h][:], spread[h][:])
+                nc.vector.transpose(wgt_sb[:, h * HALF : (h + 1) * HALF], spread[h][:])
 
         wg_w_raw = held([P, PASSES, R], I32, "wg_w_raw")
 
@@ -91,9 +91,13 @@ def tile_list_tanh_biasP_kernel(
             nc.sync.dma_start(bias[:], b.rearrange("(p t) -> p t", t=PACK))
 
         offsets = keep.tile([P, J // 16], U16, name="offsets")
-        nc.sync.dma_start(offsets[:], offs)
+
+        def load_offs():
+            nc.sync.dma_start(offsets[:], offs)
+
         load_L()
         load_x(0, 0)
+        load_offs()
         load_x(0, 1)
         load_x(0, 2)
         load_x(0, 3)
@@ -127,20 +131,20 @@ def tile_list_tanh_biasP_kernel(
 
         x_codes = [held([P, J], I32, "x_codes_%d" % a) for a in range(PASSES)]
         x_scales = [held([P, J], U8, "x_scales_%d" % a) for a in range(PASSES)]
-        picked = {(a, h): held([P, PACK, HALF], F32, "picked_%d_%d" % (a, h)) for a in range(PASSES) for h in range(2)}
+        picked = [held([P, PACK, J], F32, "picked_%d" % a) for a in range(PASSES)]
         xb = {}
 
-        def gather(a, i, h):
+        def gather(a, i, j0, width):
             nc.vector.tensor_tensor(
-                picked[a, h][:, i, :],
-                x_sb[a, i][:].indirect(offsets[:, h * HALF // 16 : (h + 1) * HALF // 16]),
-                wgt_sb[h][:],
+                picked[a][:, i, j0 : j0 + width],
+                x_sb[a, i][:].indirect(offsets[:, j0 // 16 : (j0 + width) // 16]),
+                wgt_sb[:, j0 : j0 + width],
                 MULT,
             )
 
         def round_x(copy, a, j0, width):
             xb[a, j0] = keep.tile([P, width * PACK], BF16, name="xb_%d" % width, align_bytes=64, bufs=(2 if width == HALF else 4))
-            interleave(copy, xb[a, j0][:], picked[a, j0 // HALF][:, :, j0 % HALF : j0 % HALF + width])
+            interleave(copy, xb[a, j0][:], picked[a][:, :, j0 : j0 + width])
 
         def quant_x(a, j0, width):
             quantise(x_codes[a][:, j0 : j0 + width], x_scales[a][:, j0 : j0 + width], xb[a, j0][:])
@@ -268,31 +272,25 @@ def tile_list_tanh_biasP_kernel(
                 )
 
         prep_wgt()
-        gather(0, 0, 0)
-        gather(0, 0, 1)
-        gather(0, 1, 0)
-        gather(0, 1, 1)
-        gather(0, 2, 0)
-        gather(0, 2, 1)
-        gather(0, 3, 0)
-        gather(0, 3, 1)
+        gather(0, 0, 0, 1024)
+        gather(0, 1, 0, 1024)
+        gather(0, 2, 0, 1024)
+        gather(0, 3, 0, 512)
+        gather(0, 3, 512, 512)
         round_x(S, 0, 0, 512)
         round_x(S, 0, 512, 512)
         deal_wu(S, 1)
         deal_wu(S, 0)
-        gather(1, 0, 0)
-        gather(1, 0, 1)
+        gather(1, 0, 0, 1024)
         deal_wg()
-        gather(1, 1, 0)
-        gather(1, 1, 1)
-        gather(1, 2, 0)
-        gather(1, 2, 1)
+        gather(1, 1, 0, 1024)
+        gather(1, 2, 0, 1024)
         quant_x(0, 0, 512)
         quant_x(0, 512, 512)
         quant_wu(1)
-        gather(1, 3, 0)
+        gather(1, 3, 0, 512)
         quant_wu(0)
-        gather(1, 3, 1)
+        gather(1, 3, 512, 512)
         round_x(S, 1, 0, 256)
         quant_x(1, 0, 256)
         deal_wd(V)

from contextlib import ExitStack

import concourse.mybir as mybir

K, R, N, T, J = 1024, 512, 512, 2048, 1024
FLOPS = 2 * J * (2 * K * R + R * N)

F32 = mybir.dt.float32
BF16 = mybir.dt.bfloat16
I32 = mybir.dt.int32
U16 = mybir.dt.uint16
U8 = mybir.dt.uint8
FP8X4 = mybir.dt.float8_e4m3fn_x4
MULT = mybir.AluOpType.mult
TANH = mybir.ActivationFunctionType.Tanh
IDENTITY = mybir.ActivationFunctionType.Identity

P = 128
PACK = 4
PASSES = K // (P * PACK)
HALF = J // 2
WIDE = 256
NARROW = 128


def tile_list_tanh_biasP_kernel(
    tc, xT, wgt, wg_words, wg_scales, wu, wd, b, offs, out_0, out_1, out_2
):
    nc = tc.nc
    with ExitStack() as ctx:
        keep = ctx.enter_context(tc.tile_pool(name="keep", bufs=1))
        psum = ctx.enter_context(tc.psum_pool(name="psum", bufs=1))

        def held(shape, dtype, name):
            return keep.tile(shape, dtype, name=name, align_bytes=64)

        wg_s_raw = held([P, R], U8, "wg_s_raw")
        nc.vector.memset(wg_s_raw[:].bitcast(I32), 0)

        x_planes = xT.rearrange("(a p i) t -> a i p t", p=P, i=PACK)
        x_sb = {}

        def load_x(a, i):
            x_sb[a, i] = held([P, T], F32, "x_%d_%d" % (a, i))
            nc.sync.dma_start(x_sb[a, i][:], x_planes[a, i])

        wgt_sb = held([P, J], F32, "wgt_sb")

        wgt_rows = held([P, 64], F32, "wgt_rows")

        def load_L():
            nc.sync.dma_start(wgt_rows[:], wgt.rearrange("(g r) (s c) -> r g s c", r=16, c=64)[0])

        def prep_wgt():
            turned = held([P, 64], F32, "wgt_turned")
            for e in range(2):
                nc.vector.transpose(turned[:, 32 * e : 32 * (e + 1)], wgt_rows[:, 32 * e : 32 * (e + 1)])
            by_piece = turned[:].rearrange("p (e u s) -> p s e u", e=2, u=2)
            spread = [held([P, HALF], F32, "wgt_spread_%d" % h) for h in range(2)]
            for h in range(2):
                (nc.vector.tensor_copy, nc.scalar.copy)[h](
                    spread[h][:].rearrange("p (s e u k) -> p s e u k", e=2, u=2, k=16),
                    by_piece[:, 8 * h : 8 * (h + 1)].unsqueeze(4).broadcast_to([P, 8, 2, 2, 16]),
                )
            for h in range(2):
                nc.vector.transpose(wgt_sb[:, h * HALF : (h + 1) * HALF], spread[h][:])

        wg_w_raw = held([P, PASSES, R], I32, "wg_w_raw")

        def load_wg():
            nc.sync.dma_start(wg_w_raw[:], wg_words.rearrange("a p r i -> p a (r i)").bitcast(I32))
            for q in range(4):
                nc.sync.dma_start(
                    wg_s_raw[32 * q : 32 * q + 4 * PASSES, :].bitcast(I32),
                    wg_scales[:, 4 * q : 4 * q + 4, :].bitcast(I32),
                )

        wu_rows = wu.rearrange("(a p i) r -> a p i r", p=P, i=PACK)
        wu_raw = [held([P, PACK, R], F32, "wu_raw_%d" % a) for a in range(PASSES)]

        def load_wu(a):
            nc.sync.dma_start(wu_raw[a][:], wu_rows[a])

        wd_raw = held([P, PACK, N], F32, "wd_raw")
        bias = held([P, PACK], F32, "bias")

        def load_wd():
            nc.sync.dma_start(wd_raw[:], wd.rearrange("(p i) n -> p i n", i=PACK))

        def load_bias():
            nc.sync.dma_start(bias[:], b.rearrange("(p t) -> p t", t=PACK))

        offsets = keep.tile([P, J // 16], U16, name="offsets")

        def load_offs():
            nc.sync.dma_start(offsets[:], offs)

        load_L()
        load_x(0, 0)
        load_offs()
        load_x(0, 1)
        load_x(0, 2)
        load_x(0, 3)
        load_x(1, 0)
        load_wg()
        load_wu(1)
        load_x(1, 1)
        load_x(1, 2)
        load_wu(0)
        load_x(1, 3)
        load_wd()
        load_bias()

        def quantise(codes, scales, values):
            nc.vector.quantize_mx(out=codes.bitcast(FP8X4), scales=scales, in_=values)

        def interleave(copy, dst, src):
            copy(
                dst.rearrange("p (c s t) -> p c t s", s=4, t=PACK),
                src.rearrange("p t (c s) -> p c t s", s=4),
            )

        def deal(copy, dst, raw):
            copy(
                dst.rearrange("p (t m i) -> p m i t", t=PACK, i=PACK),
                raw.rearrange("p i (m t) -> p m i t", t=PACK),
            )

        V = nc.vector.tensor_copy
        S = nc.scalar.copy

        x_codes = [held([P, J], I32, "x_codes_%d" % a) for a in range(PASSES)]
        x_scales = [held([P, J], U8, "x_scales_%d" % a) for a in range(PASSES)]
        picked = [held([P, PACK, J], F32, "picked_%d" % a) for a in range(PASSES)]
        xb = {}

        def gather(a, i, j0, width):
            nc.vector.tensor_tensor(
                picked[a][:, i, j0 : j0 + width],
                x_sb[a, i][:].indirect(offsets[:, j0 // 16 : (j0 + width) // 16]),
                wgt_sb[:, j0 : j0 + width],
                MULT,
            )

        def round_x(copy, a, j0, width):
            xb[a, j0] = keep.tile([P, width * PACK], BF16, name="xb_%d" % width, align_bytes=64, bufs=(2 if width == HALF else 4))
            interleave(copy, xb[a, j0][:], picked[a][:, :, j0 : j0 + width])

        def quant_x(a, j0, width):
            quantise(x_codes[a][:, j0 : j0 + width], x_scales[a][:, j0 : j0 + width], xb[a, j0][:])

        wg_codes = held([P, PASSES, R], I32, "wg_codes")
        wg_s = held([P, R], U8, "wg_s")

        def deal_wg():
            nc.vector.tensor_copy(
                wg_codes[:].rearrange("p a (t m) -> p a m t", t=PACK),
                wg_w_raw[:].rearrange("p a (m t) -> p a m t", t=PACK),
            )
            nc.vector.tensor_copy(
                wg_s[:].rearrange("p (t m) -> p m t", t=PACK),
                wg_s_raw[:].rearrange("p (m t) -> p m t", t=PACK),
            )

        wu_codes = [held([P, R], I32, "wu_codes_%d" % a) for a in range(PASSES)]
        wu_scales = [held([P, R], U8, "wu_scales_%d" % a) for a in range(PASSES)]
        wu_b = [held([P, R * PACK], BF16, "wu_b_%d" % a) for a in range(PASSES)]

        def deal_wu(copy, a):
            deal(copy, wu_b[a][:], wu_raw[a][:])

        def quant_wu(a):
            quantise(wu_codes[a][:], wu_scales[a][:], wu_b[a][:])

        wd_b = held([P, N * PACK], BF16, "wd_b")
        wd_codes = held([P, N], I32, "wd_codes")
        wd_scales = held([P, N], U8, "wd_scales")

        def deal_wd(copy):
            deal(copy, wd_b[:], wd_raw[:])

        def quant_wd():
            quantise(wd_codes[:], wd_scales[:], wd_b[:])

        def first_product(bank, codes, scales, j0):
            for a in range(PASSES):
                for t in range(PACK):
                    cols = slice(t * P, (t + 1) * P)
                    nc.tensor.matmul_mx(
                        out=bank[:, t, :],
                        lhsT=codes(a, cols).bitcast(FP8X4),
                        lhsT_scale=scales(a, cols),
                        rhs=x_codes[a][:, j0 : j0 + NARROW].bitcast(FP8X4),
                        rhs_scale=x_scales[a][:, j0 : j0 + NARROW],
                        start=(a == 0 and t == 0),
                        stop=(a == PASSES - 1 and t == PACK - 1),
                    )

        gate = {}
        banks_taken = []

        def next_bank(shape):
            banks_taken.append(shape)
            return psum.tile(shape, F32, name="bank_%d" % ((len(banks_taken) - 1) % 8))

        def tanh(c):
            ga = next_bank([P, PACK, NARROW])
            first_product(ga, lambda a, cols: wg_codes[:, a, cols], lambda a, cols: wg_s[4 * a :, cols], c * NARROW)
            gate[c] = keep.tile([P, NARROW, PACK], F32, name="gate", align_bytes=64, bufs=6)
            nc.scalar.activation(gate[c][:], ga[:].rearrange("p t j -> p j t"), TANH)

        h_codes = held([P, J], I32, "h_codes")
        h_scales = held([P, J], U8, "h_scales")
        y_codes = held([P, J], I32, "y_codes")
        y_scales = held([P, J], U8, "y_scales")
        out_rows = out_0.rearrange("(p t) j -> p t j", t=PACK)
        out_words = out_1[0].rearrange("p j i -> p (j i)").bitcast(I32)
        hb = held([P, J * PACK], BF16, "hb")
        yb = held([P, J * PACK], BF16, "yb")
        yf = {}

        def hidden(c):
            ub = next_bank([P, PACK, NARROW])
            first_product(ub, lambda a, cols: wu_codes[a][:, cols], lambda a, cols: wu_scales[a][:, cols], c * NARROW)
            nc.vector.tensor_tensor(
                hb[:, c * NARROW * PACK : (c + 1) * NARROW * PACK].rearrange("p (j t) -> p j t", t=PACK),
                ub[:].rearrange("p t j -> p j t"),
                gate[c][:],
                MULT,
            )

        def quant_h(j0, width):
            js = slice(j0, j0 + width)
            quantise(h_codes[:, js], h_scales[:, js], hb[:, j0 * PACK : (j0 + width) * PACK])

        def down(j0, width):
            js = slice(j0, j0 + width)
            yf[j0] = held([P, PACK, width], F32, "yf_%d" % j0)
            per_bank = min(PACK, 512 // width)
            for u in range(PACK // per_bank):
                bank = next_bank([P, per_bank, width])
                for v in range(per_bank):
                    t = per_bank * u + v
                    cols = slice(t * P, (t + 1) * P)
                    nc.tensor.matmul_mx(
                        out=bank[:, v, :],
                        lhsT=wd_codes[:, cols].bitcast(FP8X4),
                        lhsT_scale=wd_scales[:, cols],
                        rhs=h_codes[:, js].bitcast(FP8X4),
                        rhs_scale=h_scales[:, js],
                        start=True,
                        stop=True,
                    )
                for v in range(per_bank):
                    t = per_bank * u + v
                    nc.scalar.activation(yf[j0][:, t, :], bank[:, v, :], IDENTITY, bias=bias[:, t : t + 1])
            nc.sync.dma_start(out_rows[:, :, js], yf[j0][:])

        def round_y(copy, j0, width):
            interleave(copy, yb[:, j0 * PACK : (j0 + width) * PACK], yf[j0][:])

        def quant_y(j0, width):
            js = slice(j0, j0 + width)
            quantise(y_codes[:, js], y_scales[:, js], yb[:, j0 * PACK : (j0 + width) * PACK])
            nc.sync.dma_start(out_words[:, js], y_codes[:, js])

        def store_scales():
            for q in range(4):
                queue = nc.sync if q % 2 else nc.scalar
                queue.dma_start(
                    out_2[0, 4 * q : 4 * q + 4, :].bitcast(I32), y_scales[32 * q : 32 * q + 4, :].bitcast(I32)
                )

        prep_wgt()
        gather(0, 0, 0, 1024)
        gather(0, 1, 0, 1024)
        gather(0, 2, 0, 1024)
        gather(0, 3, 0, 512)
        gather(0, 3, 512, 512)
        round_x(S, 0, 0, 512)
        round_x(S, 0, 512, 512)
        deal_wu(S, 1)
        deal_wu(S, 0)
        gather(1, 0, 0, 1024)
        deal_wg()
        gather(1, 1, 0, 1024)
        gather(1, 2, 0, 1024)
        quant_x(0, 0, 512)
        quant_x(0, 512, 512)
        quant_wu(1)
        gather(1, 3, 0, 512)
        quant_wu(0)
        gather(1, 3, 512, 512)
        round_x(S, 1, 0, 256)
        quant_x(1, 0, 256)
        deal_wd(V)
        round_x(S, 1, 256, 256)
        quant_x(1, 256, 256)
        quant_wd()
        round_x(S, 1, 512, 256)
        quant_x(1, 512, 256)
        tanh(0)
        tanh(1)
        tanh(2)
        tanh(3)
        round_x(S, 1, 768, 256)
        quant_x(1, 768, 256)
        hidden(0)
        hidden(1)
        quant_h(0, 256)
        hidden(2)
        hidden(3)
        quant_h(256, 256)
        tanh(4)
        tanh(5)
        down(0, 256)
        round_y(V, 0, 256)
        quant_y(0, 256)
        hidden(4)
        hidden(5)
        quant_h(512, 256)
        tanh(6)
        tanh(7)
        down(256, 256)
        round_y(V, 256, 256)
        quant_y(256, 256)
        hidden(6)
        hidden(7)
        quant_h(768, 256)
        down(512, 256)
        round_y(V, 512, 256)
        quant_y(512, 256)
        down(768, 256)
        round_y(V, 768, 256)
        quant_y(768, 256)
        store_scales()
